import numpy as np
import ml_dtypes


def mxq(x, axis, fmt="e4m3"):
    dtype, down = {"e4m3": (ml_dtypes.float8_e4m3fn, 7), "e5m2": (ml_dtypes.float8_e5m2, 14)}[fmt]
    v = np.moveaxis(np.asarray(x, np.float32).astype(ml_dtypes.bfloat16).astype(np.float64), axis, -1)
    blocks = v.reshape(v.shape[:-1] + (-1, 32))
    amax = np.abs(blocks).max(-1, keepdims=True)
    byte = np.maximum(np.where(amax > 0, np.frexp(amax)[1] - 1 + 127, 0) - down, 1)
    scale = np.exp2(byte - 127.0)
    codes = (blocks / scale).astype(np.float32).astype(dtype).astype(np.float64)
    return np.moveaxis((codes * scale).reshape(v.shape), -1, axis)


WIDE = False


def mx_kscale(k):
    if not WIDE:
        return np.ones(k)
    levels = np.array([10, -10, 5, -5, 0])
    if k % 512:
        return np.exp2(np.random.permutation(np.resize(levels, k // 32))).repeat(32)
    a = np.empty((k // 512, 16))
    for p in range(k // 512):
        a[p, :8] = np.random.permutation(np.resize(levels, 8))
        for g in range(8):
            far = levels[np.abs(levels - a[p, g]) >= 10]
            a[p, g + 8] = far[np.random.randint(len(far))]
    return np.exp2(a.ravel()).repeat(32)


def f64(x):
    return np.asarray(x).astype(np.float64)


def striped(idx):
    return np.tile(np.asarray(idx).reshape(-1, 16).T, (8, 1)).astype(np.uint16)


def unstriped(offs):
    return offs[:16].T.reshape(-1).astype(np.int64)


E2M1 = np.array([0.0, 0.5, 1.0, 1.5, 2.0, 3.0, 4.0, 6.0, -0.0, -0.5, -1.0, -1.5, -2.0, -3.0, -4.0, -6.0])


def pack_weight(w, fmt):
    k, n = w.shape
    w = f64(np.asarray(w, np.float32).astype(ml_dtypes.bfloat16)).reshape(k // 32, 32, n)
    amax = np.abs(w).max(1)
    if fmt == "e4m3":
        byte = np.frexp(amax)[1] - 1 + 127 - 7
    else:
        mant, ex = np.frexp(amax / 6.0)
        byte = np.where(mant > 0.5, ex, ex - 1) + 127
    byte = np.clip(np.where(amax > 0, byte, 1), 1, 254)
    scaled = (w * np.exp2(127.0 - byte)[:, None, :]).reshape(k, n).astype(np.float32)
    by_word = np.ascontiguousarray(scaled.reshape(k // 512, 128, 4, n).transpose(0, 1, 3, 2))
    if fmt == "e4m3":
        words = by_word.astype(ml_dtypes.float8_e4m3fn).view(np.uint8)
    else:
        c = by_word.astype(ml_dtypes.float4_e2m1fn).view(np.uint8) & 0xF
        words = (c[..., 0::2] | (c[..., 1::2] << 4)).reshape(k // 512, 128, 2 * n)
    return np.ascontiguousarray(words), np.ascontiguousarray(byte.astype(np.uint8).reshape(k // 512, 16, n))


def unpack_weight(words, scales, fmt):
    g, _, n = scales.shape
    words = np.ascontiguousarray(words).reshape(g, 128, n, -1)
    if fmt == "e4m3":
        vals = words.view(ml_dtypes.float8_e4m3fn).astype(np.float64)
    else:
        nib = np.empty((g, 128, n, 4), np.uint8)
        nib[..., 0::2] = words & 0xF
        nib[..., 1::2] = words >> 4
        vals = E2M1[nib]
    vals = vals * np.repeat(np.exp2(scales.astype(np.float64) - 127.0), 8, axis=1)[..., None]
    return vals.transpose(0, 1, 3, 2).reshape(g * 512, n)


B, N, T, D, DV, NQ = 1, 512, 2048, 1024, 256, 128
DRAFT = 128


def setup_inputs():
    n = np.random.standard_normal
    idx = np.random.permutation(T)[:B * N]
    s = mx_kscale(D)[:, None]
    u = np.ones(T)
    u[idx] = mx_kscale(B * N)
    r = np.random.uniform(0.5, 2.0, T)
    qp = [pack_weight(x, "e4m3") for x in n((B, D, NQ)) * s * (0.80 / np.sqrt(D))]
    k = n((D, T)) / s
    v = n((DV, T)) / (u * r)
    kp = pack_weight(k, "e2m1")
    when = np.zeros(T)
    when[idx] = np.concatenate([np.concatenate([np.arange(N - DRAFT), N - DRAFT + np.random.randint(0, 16, DRAFT)]) for b in range(B)])
    return {
        "q_words": np.stack([x[0] for x in qp]),
        "q_scales": np.stack([x[1] for x in qp]),
        "k_words": np.ascontiguousarray(kp[0].reshape(D // 1024, 2, 128, T, 2).transpose(0, 2, 3, 1, 4)).reshape(D // 1024, 128, T, 4),
        "k_scales": kp[1],
        "vT": v.astype(np.float32),
        "vs": np.tile(u * r, (128, 1)).astype(np.float32),
        "pos": np.tile(when, (128, 1)).astype(np.float32),
        "qpos": np.random.randint(N - DRAFT, N - DRAFT + 16, (B, NQ, 1)).astype(np.float32),
        "sink": (2.0 + 3.0 * n((B, NQ, 1))).astype(np.float32),
        "offs": striped(idx),
    }


def reference(q_words, q_scales, k_words, k_scales, vT, vs, pos, qpos, sink, offs):
    idx = unstriped(offs)
    k = unpack_weight(k_words.reshape(D // 1024, 128, T, 2, 2).transpose(0, 3, 1, 2, 4).reshape(D // 512, 128, 2 * T), k_scales, "e2m1")
    v = f64(vT)
    pick = lambda x: x[:, idx].reshape(x.shape[0], B, N).transpose(1, 0, 2)
    q = np.stack([unpack_weight(q_words[b], q_scales[b], "e4m3") for b in range(B)])
    score = q.transpose(0, 2, 1) @ pick(k)
    score = np.where(pick(f64(pos))[:, :1, :] <= f64(qpos), score, -30000.0)
    m = np.maximum(score.max(-1, keepdims=True), f64(sink))
    p = np.exp(score - m)
    total = p.sum(-1, keepdims=True) + np.exp(f64(sink) - m)
    w = p * pick(f64(vs))[:, :1, :]
    y = mxq(w, 2, "e4m3") @ mxq(pick(v).transpose(0, 2, 1), 1, "e4m3")
    y = y / total
    return y

@@ -1,0 +1,221 @@
+from contextlib import ExitStack
+
+import concourse.mybir as mybir
+from concourse.masks import make_identity
+
+P = 128
+N, T, D, DV, NQ = 512, 2048, 1024, 256, 128
+PACK = 4
+PASSES = D // (P * PACK)
+HALVES = DV // P
+FLOPS = 2 * NQ * N * (D + DV)
+BYTES = P * T * 4 + 32 * T + D * NQ + 32 * NQ + DV * T * 4 + 2 * T * 4 + 2 * NQ * 4 + P * 64 + NQ * DV * 4
+
+F32 = mybir.dt.float32
+BF16 = mybir.dt.bfloat16
+I32 = mybir.dt.int32
+U32 = mybir.dt.uint32
+U16 = mybir.dt.uint16
+U8 = mybir.dt.uint8
+FP8X4 = mybir.dt.float8_e4m3fn_x4
+FP4X4 = mybir.dt.float4_e2m1fn_x4
+ALU = mybir.AluOpType
+ACT = mybir.ActivationFunctionType
+
+MASKED = 30000.0
+STEEP = 2.0 ** 60
+SHIFT = 16
+
+
+def tile_attend_soft_draft_sink_topkq128n512t2048_kernel(
+    tc, q_words, q_scales, k_words, k_scales, vT, vs, pos, qpos, sink, offs, out
+):
+    nc = tc.nc
+    with ExitStack() as ctx:
+        keep = ctx.enter_context(tc.tile_pool(name="keep", bufs=1))
+        psum = ctx.enter_context(tc.psum_pool(name="psum", bufs=1))
+
+        offsets = keep.tile([P, N // 16], U16, name="offsets")
+        nc.sync.dma_start(offsets[:], offs)
+        listed = offsets[:]
+
+        key_pool = keep.tile([P, T], I32, name="key_pool")
+        nc.sync.dma_start(key_pool[:], k_words[0].rearrange("g t b -> g (t b)").bitcast(I32))
+
+        kscale_pool = keep.tile([P, T], U8, name="kscale_pool", tag="pool_a")
+        nc.vector.memset(kscale_pool[:].bitcast(I32), 0)
+        krows = k_scales.rearrange("o (c r) t -> r c o t", r=4)
+        for r in range(4):
+            nc.scalar.dma_start(kscale_pool[r::SHIFT, :].bitcast(I32), krows[r].bitcast(I32))
+
+        pos_pool = keep.tile([P, T], F32, name="pos_pool", tag="pool_b")
+        nc.vector.memset(pos_pool[:].bitcast(I32), 0)
+        nc.scalar.dma_start(pos_pool[0:1, :], pos[0:1, :])
+
+        warm = keep.tile([P, 1], F32, name="warm")
+        nc.vector.memset(warm[:], 0.0)
+        nc.scalar.activation(warm[:], warm[:], ACT.Exp)
+
+        q_codes = keep.tile([P, PASSES, NQ], I32, name="q_codes", align_bytes=64)
+        nc.scalar.dma_start(q_codes[:], q_words[0].rearrange("o g q r -> g o (q r)").bitcast(I32))
+        qpos_col = keep.tile([P, 1], F32, name="qpos_col")
+        nc.scalar.dma_start(qpos_col[:], qpos[0])
+
+        ident = keep.tile([P, P], F32, name="ident")
+        make_identity(nc, ident[:])
+
+        vs_pool = keep.tile([P, T], F32, name="vs_pool")
+        nc.gpsimd.memset(vs_pool[:], 0.0)
+        nc.scalar.dma_start(vs_pool[0:1, :], vs[0:1, :])
+        sink_col = keep.tile([P, 1], F32, name="sink_col")
+        nc.gpsimd.dma_start(sink_col[:], sink[0])
+        ident_bf = keep.tile([P, P], BF16, name="ident_bf")
+        nc.scalar.copy(ident_bf[:], ident[:])
+
+        q_plane = keep.tile([P, PASSES * NQ], U8, name="q_plane", align_bytes=64)
+        nc.vector.memset(q_plane[:].bitcast(I32), 0)
+        qrows = q_scales[0].rearrange("o (c r) q -> r c o q", r=4)
+        for r in range(4):
+            nc.sync.dma_start(
+                q_plane[r::32, :].bitcast(I32).rearrange("c (o q) -> c o q", o=PASSES),
+                qrows[r].bitcast(I32),
+            )
+
+        kscale_both = keep.tile([P, N], U8, name="kscale_both", align_bytes=64)
+        nc.vector.tensor_copy(kscale_both[:], kscale_pool[:].indirect(listed))
+        kscale_second = keep.tile([P, N], U8, name="kscale_second", align_bytes=64)
+        nc.vector.memset(kscale_second[:].bitcast(I32), 0)
+        nc.scalar.dma_start(
+            kscale_second[0 : P - SHIFT, :].bitcast(I32), kscale_both[SHIFT:P, :].bitcast(I32)
+        )
+        k_planes = [kscale_both, kscale_second]
+
+        pos_row = keep.tile([P, N], F32, name="pos_row")
+        nc.vector.tensor_copy(pos_row[:], pos_pool[:].indirect(listed))
+
+        value_pools = []
+        for h, tag in enumerate(("pool_a", "pool_b")):
+            value_pool = keep.tile([P, T], F32, name="value_pool%d" % h, tag=tag)
+            nc.sync.dma_start(value_pool[:], vT[h * P : (h + 1) * P, :])
+            value_pools.append(value_pool)
+
+        neg_qpos = keep.tile([P, 1], F32, name="neg_qpos")
+        nc.scalar.activation(neg_qpos[:], qpos_col[:], ACT.Copy, scale=-1.0)
+        neg_score = keep.tile([P, N + 8], F32, name="neg_score")
+        nc.scalar.activation(neg_score[:, N : N + 1], sink_col[:], ACT.Copy, scale=-1.0)
+
+        pos_turned = psum.tile([P, 4, P], F32, name="pos_turned", tag="bank_a")
+        for j in range(4):
+            nc.tensor.transpose(pos_turned[:, j, :], pos_row[:, j * P : (j + 1) * P], ident[:])
+        pos_cols = keep.tile([P, 4], F32, name="pos_cols")
+        nc.scalar.copy(pos_cols[:], pos_turned[:, :, 0])
+        pos_wide = psum.tile([P, N], F32, name="pos_wide", tag="bank_b")
+        for j in range(4):
+            nc.tensor.transpose(
+                pos_wide[:, j * P : (j + 1) * P], pos_cols[:, j : j + 1].to_broadcast([P, P]), ident[:]
+            )
+        ahead = keep.tile([P, N], F32, name="ahead")
+        nc.scalar.activation(
+            ahead[:].rearrange("q (t s) -> q t s", t=PACK),
+            pos_wide[:].rearrange("q (s t) -> q t s", t=PACK),
+            ACT.Relu,
+            bias=neg_qpos[:],
+        )
+
+        key_pairs = keep.tile([P, N], U32, name="key_pairs")
+        nc.vector.tensor_copy(key_pairs[:], key_pool[:].bitcast(U32).indirect(listed))
+        score = psum.tile([P, N], F32, name="score")
+        for o in range(PASSES):
+            key_codes = keep.tile([P, 2 * N], U8, name="key_codes%d" % o, align_bytes=64)
+            nc.vector.tensor_copy(key_codes[:].bitcast(U16), key_pairs[:].bitcast(U16)[:, o::2])
+            nc.tensor.matmul_mx(
+                score[:],
+                lhsT=q_codes[:, o, :].bitcast(FP8X4),
+                lhsT_scale=q_plane[:, o * NQ : (o + 1) * NQ],
+                rhs=key_codes[:].bitcast(FP4X4),
+                rhs_scale=k_planes[o][:],
+                start=(o == 0),
+                stop=(o == PASSES - 1),
+            )
+
+        vs_row = keep.tile([P, N], F32, name="vs_row")
+        nc.vector.tensor_copy(vs_row[:], vs_pool[:].indirect(listed))
+        vs_turned = psum.tile([P, PACK, P], F32, name="vs_turned")
+        for t in range(PACK):
+            nc.tensor.transpose(vs_turned[:, t, :], vs_row[:, t::PACK], ident[:])
+        vs_cols = keep.tile([P, PACK], F32, name="vs_cols")
+        nc.scalar.copy(vs_cols[:], vs_turned[:, :, 0])
+
+        neg_raw = keep.tile([P, N], F32, name="neg_raw")
+        nc.vector.scalar_tensor_tensor(
+            neg_raw[:].rearrange("q (t s) -> q t s", t=PACK),
+            ahead[:].rearrange("q (t s) -> q t s", t=PACK),
+            STEEP,
+            score[:].rearrange("q (s t) -> q t s", t=PACK),
+            ALU.mult,
+            ALU.subtract,
+        )
+        neg_max = keep.tile([P, 1], F32, name="neg_max")
+        nc.vector.tensor_scalar(
+            neg_score[:, 0:N], neg_raw[:], MASKED, neg_score[:, N : N + 1], ALU.min, ALU.min, accum_out=neg_max[:]
+        )
+        prob = keep.tile([P, N + 8], F32, name="prob")
+        total = keep.tile([P, 1], F32, name="total")
+        nc.scalar.activation(
+            prob[:, 0 : N + 1], neg_score[:, 0 : N + 1], ACT.Exp, bias=neg_max[:], scale=-1.0, accum_out=total[:]
+        )
+        prob_turned = psum.tile([P, PACK, NQ], F32, name="prob_turned")
+        for t in range(PACK):
+            nc.tensor.transpose(prob_turned[:, t, :], prob[:, t * P : (t + 1) * P], ident[:])
+
+        v_codes, v_planes = [], []
+        v_packed = []
+        for h in range(HALVES):
+            picked = keep.tile([P, N], BF16, name="picked%d" % h)
+            nc.vector.tensor_copy(picked[:], value_pools[h][:].indirect(listed))
+            turned = psum.tile([P, PACK, P], BF16, name="turned%d" % h)
+            for t in range(PACK):
+                nc.tensor.transpose(turned[:, t, :], picked[:, t::PACK], ident_bf[:])
+            packed = keep.tile([P, P, PACK], BF16, name="packed%d" % h, align_bytes=64)
+            nc.scalar.copy(packed[:], turned[:].rearrange("s t e -> s e t"))
+            v_packed.append(packed)
+
+        weight = keep.tile([P, NQ, PACK], BF16, name="weight", align_bytes=64)
+        nc.vector.tensor_tensor(
+            weight[:],
+            prob_turned[:].rearrange("s t q -> s q t"),
+            vs_cols[:].unsqueeze(1).to_broadcast([P, NQ, PACK]),
+            ALU.mult,
+        )
+        inverse = keep.tile([P, 1], F32, name="inverse")
+        nc.vector.reciprocal(inverse[:], total[:])
+
+        def quantise(values, name):
+            codes = keep.tile([P, P], U32, name=name + "_codes", align_bytes=64)
+            plane = keep.tile([P, P], U8, name=name + "_plane", align_bytes=64)
+            nc.vector.quantize_mx(codes[:].bitcast(FP8X4), plane[:], values[:].rearrange("s c t -> s (c t)"))
+            return codes, plane
+
+        quantised = [quantise(v_packed[0], "v0")]
+        w_codes, w_plane = quantise(weight, "w")
+        quantised.append(quantise(v_packed[1], "v1"))
+
+        for h, tag in enumerate(("bank_a", "bank_b")):
+            codes, plane = quantised[h]
+            acc = psum.tile([NQ, P], F32, name="acc%d" % h, tag=tag)
+            nc.tensor.matmul_mx(
+                acc[:],
+                lhsT=w_codes[:].bitcast(FP8X4),
+                lhsT_scale=w_plane[:],
+                rhs=codes[:].bitcast(FP8X4),
+                rhs_scale=plane[:],
+                start=True,
+                stop=True,
+            )
+            result = keep.tile([NQ, P], F32, name="result%d" % h)
+            if h == 0:
+                nc.scalar.activation(result[:], acc[:], ACT.Copy, scale=inverse[:])
+                nc.scalar.dma_start(out[0][:, h * P : (h + 1) * P], result[:])
+            else:
+                nc.vector.tensor_scalar(result[:], acc[:], inverse[:], None, ALU.mult)
+                nc.sync.dma_start(out[0][:, h * P : (h + 1) * P], result[:])

@@ -24,7 +24,16 @@ ACT = mybir.ActivationFunctionType
 
 MASKED = 30000.0
 STEEP = 2.0 ** 60
-SHIFT = 16
+LOW = 96
+ROW = P - 1
+
+
+def in_order(row):
+    return row.rearrange("x (b t r) -> x b t r", t=PACK, r=8)
+
+
+def dealt(row):
+    return row.rearrange("x (t b r) -> x b t r", t=PACK, r=8)
 
 
 def tile_attend_soft_draft_sink_topkq128n512t2048_kernel(
@@ -39,38 +48,24 @@ def tile_attend_soft_draft_sink_topkq128n512t2048_kernel(
         nc.sync.dma_start(offsets[:], offs)
         listed = offsets[:]
 
-        key_pool = keep.tile([P, T], I32, name="key_pool")
+        kscale_pool = keep.tile([P, T], U8, name="kscale_pool")
+        nc.sync.dma_start(kscale_pool[LOW:P, :].bitcast(I32), k_scales.rearrange("o f t -> f o t").bitcast(I32))
+        pos_parts = keep.tile([P, 4, 4], F32, name="pos_parts", tag="chain_e")
+        nc.scalar.dma_start(pos_parts[:], pos[0].rearrange("(p b i) -> p b i", b=4, i=4))
+        vs_pool = keep.tile([P, T], F32, name="vs_pool", tag="chain_c", align_bytes=64)
+        nc.sync.dma_start(vs_pool[ROW:P, :], vs[0:1, :])
+        qpos_col = keep.tile([P, 1], F32, name="qpos_col")
+        nc.scalar.dma_start(qpos_col[:], qpos[0])
+        q_codes = keep.tile([P, PASSES, NQ], I32, name="q_codes", align_bytes=64)
+        nc.scalar.dma_start(q_codes[:], q_words[0].rearrange("o g q r -> g o (q r)").bitcast(I32))
+        sink_col = keep.tile([P, 1], F32, name="sink_col")
+        nc.scalar.dma_start(sink_col[:], sink[0])
+        key_pool = keep.tile([P, T], I32, name="key_pool", tag="chain_b", align_bytes=64)
         nc.sync.dma_start(key_pool[:], k_words[0].rearrange("g t b -> g (t b)").bitcast(I32))
-
-        kscale_pool = keep.tile([P, T], U8, name="kscale_pool", tag="pool_a")
-        nc.vector.memset(kscale_pool[:].bitcast(I32), 0)
-        krows = k_scales.rearrange("o (c r) t -> r c o t", r=4)
-        for r in range(4):
-            nc.scalar.dma_start(kscale_pool[r::SHIFT, :].bitcast(I32), krows[r].bitcast(I32))
-
-        pos_pool = keep.tile([P, T], F32, name="pos_pool", tag="pool_b")
-        nc.vector.memset(pos_pool[:].bitcast(I32), 0)
-        nc.scalar.dma_start(pos_pool[0:1, :], pos[0:1, :])
 
         warm = keep.tile([P, 1], F32, name="warm")
         nc.vector.memset(warm[:], 0.0)
         nc.scalar.activation(warm[:], warm[:], ACT.Exp)
-
-        q_codes = keep.tile([P, PASSES, NQ], I32, name="q_codes", align_bytes=64)
-        nc.scalar.dma_start(q_codes[:], q_words[0].rearrange("o g q r -> g o (q r)").bitcast(I32))
-        qpos_col = keep.tile([P, 1], F32, name="qpos_col")
-        nc.scalar.dma_start(qpos_col[:], qpos[0])
-
-        ident = keep.tile([P, P], F32, name="ident")
-        make_identity(nc, ident[:])
-
-        vs_pool = keep.tile([P, T], F32, name="vs_pool")
-        nc.gpsimd.memset(vs_pool[:], 0.0)
-        nc.scalar.dma_start(vs_pool[0:1, :], vs[0:1, :])
-        sink_col = keep.tile([P, 1], F32, name="sink_col")
-        nc.gpsimd.dma_start(sink_col[:], sink[0])
-        ident_bf = keep.tile([P, P], BF16, name="ident_bf")
-        nc.scalar.copy(ident_bf[:], ident[:])
 
         q_plane = keep.tile([P, PASSES * NQ], U8, name="q_plane", align_bytes=64)
         nc.vector.memset(q_plane[:].bitcast(I32), 0)
@@ -80,107 +75,113 @@ def tile_attend_soft_draft_sink_topkq128n512t2048_kernel(
                 q_plane[r::32, :].bitcast(I32).rearrange("c (o q) -> c o q", o=PASSES),
                 qrows[r].bitcast(I32),
             )
+        first_values = keep.tile([P, T], F32, name="first_values", tag="chain_a", align_bytes=64)
+        nc.sync.dma_start(first_values[:], vT[0:P, :])
+        nc.vector.memset(kscale_pool[0:LOW, :].bitcast(I32), 0)
+        k_plane = keep.tile([P, PASSES * N], U8, name="k_plane", align_bytes=64)
+        nc.vector.memset(k_plane[:].bitcast(I32), 0)
+        nc.vector.memset(vs_pool[0:ROW, :].bitcast(I32), 0)
 
-        kscale_both = keep.tile([P, N], U8, name="kscale_both", align_bytes=64)
-        nc.vector.tensor_copy(kscale_both[:], kscale_pool[:].indirect(listed))
-        kscale_second = keep.tile([P, N], U8, name="kscale_second", align_bytes=64)
-        nc.vector.memset(kscale_second[:].bitcast(I32), 0)
-        nc.scalar.dma_start(
-            kscale_second[0 : P - SHIFT, :].bitcast(I32), kscale_both[SHIFT:P, :].bitcast(I32)
-        )
-        k_planes = [kscale_both, kscale_second]
-
-        pos_row = keep.tile([P, N], F32, name="pos_row")
-        nc.vector.tensor_copy(pos_row[:], pos_pool[:].indirect(listed))
-
-        value_pools = []
-        for h, tag in enumerate(("pool_a", "pool_b")):
-            value_pool = keep.tile([P, T], F32, name="value_pool%d" % h, tag=tag)
-            nc.sync.dma_start(value_pool[:], vT[h * P : (h + 1) * P, :])
-            value_pools.append(value_pool)
-
+        ident = keep.tile([P, P], F32, name="ident")
+        make_identity(nc, ident[:])
         neg_qpos = keep.tile([P, 1], F32, name="neg_qpos")
         nc.scalar.activation(neg_qpos[:], qpos_col[:], ACT.Copy, scale=-1.0)
-        neg_score = keep.tile([P, N + 8], F32, name="neg_score")
-        nc.scalar.activation(neg_score[:, N : N + 1], sink_col[:], ACT.Copy, scale=-1.0)
 
-        pos_turned = psum.tile([P, 4, P], F32, name="pos_turned", tag="bank_a")
-        for j in range(4):
-            nc.tensor.transpose(pos_turned[:, j, :], pos_row[:, j * P : (j + 1) * P], ident[:])
-        pos_cols = keep.tile([P, 4], F32, name="pos_cols")
-        nc.scalar.copy(pos_cols[:], pos_turned[:, :, 0])
-        pos_wide = psum.tile([P, N], F32, name="pos_wide", tag="bank_b")
-        for j in range(4):
-            nc.tensor.transpose(
-                pos_wide[:, j * P : (j + 1) * P], pos_cols[:, j : j + 1].to_broadcast([P, P]), ident[:]
+        pos_pool = keep.tile([P, T], F32, name="pos_pool", tag="chain_d", align_bytes=64)
+        for b in range(4):
+            spread = psum.tile([P, 4, P], F32, name="spread%d" % b, tag="bank%d" % b)
+            for i in range(4):
+                nc.tensor.transpose(spread[:, i, :], pos_parts[:, b, i : i + 1].to_broadcast([P, P]), ident[:])
+            nc.scalar.copy(
+                pos_pool[:].rearrange("q (p b i) -> q b p i", b=4, i=4)[:, b],
+                spread[:].rearrange("q i p -> q p i"),
             )
-        ahead = keep.tile([P, N], F32, name="ahead")
-        nc.scalar.activation(
-            ahead[:].rearrange("q (t s) -> q t s", t=PACK),
-            pos_wide[:].rearrange("q (s t) -> q t s", t=PACK),
-            ACT.Relu,
-            bias=neg_qpos[:],
-        )
+
+        kscale_rows = keep.tile([P, N], U8, name="kscale_rows")
+        nc.vector.tensor_copy(kscale_rows[:], kscale_pool[:].indirect(listed))
+        for c in range(4):
+            nc.sync.dma_start(
+                k_plane[32 * c : 32 * c + 4, :].bitcast(I32).rearrange("r (o n) -> r o n", o=PASSES),
+                kscale_rows[LOW + 8 * c : LOW + 8 * c + 8, :].bitcast(I32),
+            )
+
+        vs_row = keep.tile([P, N], F32, name="vs_row")
+        nc.vector.tensor_copy(vs_row[:], vs_pool[:].indirect(listed))
+        vs_dealt = keep.tile([P, N], F32, name="vs_dealt", tag="chain_e")
+        nc.scalar.copy(dealt(vs_dealt[:]), in_order(vs_row[:]))
+        vs_turned = psum.tile([P, PACK, P], F32, name="vs_turned", tag="bank3")
+        for t in range(PACK):
+            nc.tensor.transpose(vs_turned[:, t, :], vs_dealt[:, t * P : (t + 1) * P], ident[:])
+        vs_cols = keep.tile([P, PACK], F32, name="vs_cols")
+        nc.scalar.copy(vs_cols[:], vs_turned[:, :, ROW])
+
+        second_values = keep.tile([P, T], F32, name="second_values", tag="chain_c", align_bytes=64)
+        nc.sync.dma_start(second_values[:], vT[P : 2 * P, :])
+        value_pools = [first_values, second_values]
+
+        neg_score = keep.tile([P, N + 8], F32, name="neg_score", tag="row2", align_bytes=64)
+        nc.scalar.activation(neg_score[:, N : N + 1], sink_col[:], ACT.Copy, scale=-1.0)
 
         key_pairs = keep.tile([P, N], U32, name="key_pairs")
         nc.vector.tensor_copy(key_pairs[:], key_pool[:].bitcast(U32).indirect(listed))
         score = psum.tile([P, N], F32, name="score")
         for o in range(PASSES):
-            key_codes = keep.tile([P, 2 * N], U8, name="key_codes%d" % o, align_bytes=64)
+            key_codes = keep.tile([P, 2 * N], U8, name="key_codes%d" % o, tag="key_codes%d" % o, align_bytes=64)
             nc.vector.tensor_copy(key_codes[:].bitcast(U16), key_pairs[:].bitcast(U16)[:, o::2])
             nc.tensor.matmul_mx(
                 score[:],
                 lhsT=q_codes[:, o, :].bitcast(FP8X4),
                 lhsT_scale=q_plane[:, o * NQ : (o + 1) * NQ],
                 rhs=key_codes[:].bitcast(FP4X4),
-                rhs_scale=k_planes[o][:],
+                rhs_scale=k_plane[:, o * N : (o + 1) * N],
                 start=(o == 0),
                 stop=(o == PASSES - 1),
             )
 
-        vs_row = keep.tile([P, N], F32, name="vs_row")
-        nc.vector.tensor_copy(vs_row[:], vs_pool[:].indirect(listed))
-        vs_turned = psum.tile([P, PACK, P], F32, name="vs_turned")
-        for t in range(PACK):
-            nc.tensor.transpose(vs_turned[:, t, :], vs_row[:, t::PACK], ident[:])
-        vs_cols = keep.tile([P, PACK], F32, name="vs_cols")
-        nc.scalar.copy(vs_cols[:], vs_turned[:, :, 0])
+        pos_row = keep.tile([P, N], F32, name="pos_row", tag="chain_b", align_bytes=64)
+        nc.vector.tensor_copy(pos_row[:], pos_pool[:].indirect(listed))
+        ahead = keep.tile([P, N], F32, name="ahead")
+        nc.scalar.activation(ahead[:], pos_row[:], ACT.Relu, bias=neg_qpos[:])
 
-        neg_raw = keep.tile([P, N], F32, name="neg_raw")
-        nc.vector.scalar_tensor_tensor(
-            neg_raw[:].rearrange("q (t s) -> q t s", t=PACK),
-            ahead[:].rearrange("q (t s) -> q t s", t=PACK),
-            STEEP,
-            score[:].rearrange("q (s t) -> q t s", t=PACK),
-            ALU.mult,
-            ALU.subtract,
-        )
-        neg_max = keep.tile([P, 1], F32, name="neg_max")
+
+        def pick_values(h, slot, identity_slot):
+            picked = keep.tile([P, N], BF16, name="picked%d" % h, tag=slot, align_bytes=64)
+            nc.vector.tensor_copy(dealt(picked[:]), value_pools[h][:].indirect(listed))
+            ident_bf = keep.tile([P, P], BF16, name="ident_bf%d" % h, tag=identity_slot, align_bytes=64)
+            nc.scalar.copy(ident_bf[:], ident[:])
+            turned = psum.tile([P, PACK, P], BF16, name="turned%d" % h, tag="bank%d" % (2 - 2 * h))
+            for t in range(PACK):
+                nc.tensor.transpose(turned[:, t, :], picked[:, t * P : (t + 1) * P], ident_bf[:])
+            packed = keep.tile([P, P, PACK], BF16, name="packed%d" % h, align_bytes=64)
+            nc.scalar.copy(packed[:], turned[:].rearrange("s t e -> s e t"))
+            return packed
+
+        v_packed = [pick_values(0, "chain_d", "key_codes1")]
+
+        neg_raw = keep.tile([P, N], F32, name="neg_raw", tag="chain_a", align_bytes=64)
+        nc.vector.scalar_tensor_tensor(neg_raw[:], ahead[:], STEEP, score[:], ALU.mult, ALU.subtract)
+        neg_max = keep.tile([P, 1], F32, name="neg_max", tag="v0_plane", align_bytes=64)
         nc.vector.tensor_scalar(
-            neg_score[:, 0:N], neg_raw[:], MASKED, neg_score[:, N : N + 1], ALU.min, ALU.min, accum_out=neg_max[:]
+            dealt(neg_score[:, 0:N]),
+            in_order(neg_raw[:]),
+            MASKED,
+            neg_score[:, N : N + 1],
+            ALU.min,
+            ALU.min,
+            accum_out=neg_max[:],
         )
         prob = keep.tile([P, N + 8], F32, name="prob")
         total = keep.tile([P, 1], F32, name="total")
         nc.scalar.activation(
             prob[:, 0 : N + 1], neg_score[:, 0 : N + 1], ACT.Exp, bias=neg_max[:], scale=-1.0, accum_out=total[:]
         )
-        prob_turned = psum.tile([P, PACK, NQ], F32, name="prob_turned")
+        prob_turned = psum.tile([P, PACK, NQ], F32, name="prob_turned", tag="bank1")
         for t in range(PACK):
             nc.tensor.transpose(prob_turned[:, t, :], prob[:, t * P : (t + 1) * P], ident[:])
 
-        v_codes, v_planes = [], []
-        v_packed = []
-        for h in range(HALVES):
-            picked = keep.tile([P, N], BF16, name="picked%d" % h)
-            nc.vector.tensor_copy(picked[:], value_pools[h][:].indirect(listed))
-            turned = psum.tile([P, PACK, P], BF16, name="turned%d" % h)
-            for t in range(PACK):
-                nc.tensor.transpose(turned[:, t, :], picked[:, t::PACK], ident_bf[:])
-            packed = keep.tile([P, P, PACK], BF16, name="packed%d" % h, align_bytes=64)
-            nc.scalar.copy(packed[:], turned[:].rearrange("s t e -> s e t"))
-            v_packed.append(packed)
+        v_packed.append(pick_values(1, "chain_a", "row2"))
 
-        weight = keep.tile([P, NQ, PACK], BF16, name="weight", align_bytes=64)
+        weight = keep.tile([P, NQ, PACK], BF16, name="weight", tag="chain_c", align_bytes=64)
         nc.vector.tensor_tensor(
             weight[:],
             prob_turned[:].rearrange("s t q -> s q t"),
@@ -192,7 +193,7 @@ def tile_attend_soft_draft_sink_topkq128n512t2048_kernel(
 
         def quantise(values, name):
             codes = keep.tile([P, P], U32, name=name + "_codes", align_bytes=64)
-            plane = keep.tile([P, P], U8, name=name + "_plane", align_bytes=64)
+            plane = keep.tile([P, P], U8, name=name + "_plane", tag=name + "_plane", align_bytes=64)
             nc.vector.quantize_mx(codes[:].bitcast(FP8X4), plane[:], values[:].rearrange("s c t -> s (c t)"))
             return codes, plane
 

@@ -29,11 +29,15 @@ ROW = P - 1
 
 
 def in_order(row):
-    return row.rearrange("x (b t r) -> x b t r", t=PACK, r=8)
+    return row.rearrange("x (b u k) -> x b u k", u=2, k=16)
 
 
 def dealt(row):
-    return row.rearrange("x (t b r) -> x b t r", t=PACK, r=8)
+    return row.rearrange("x (u b k) -> x b u k", u=2, k=16)
+
+
+def place(row, t):
+    return row[:, (t // 2) * (N // 2) + t % 2 : (t // 2 + 1) * (N // 2) : 2]
 
 
 def tile_attend_soft_draft_sink_topkq128n512t2048_kernel(
@@ -111,7 +115,7 @@ def tile_attend_soft_draft_sink_topkq128n512t2048_kernel(
         nc.scalar.copy(dealt(vs_dealt[:]), in_order(vs_row[:]))
         vs_turned = psum.tile([P, PACK, P], F32, name="vs_turned", tag="bank3")
         for t in range(PACK):
-            nc.tensor.transpose(vs_turned[:, t, :], vs_dealt[:, t * P : (t + 1) * P], ident[:])
+            nc.tensor.transpose(vs_turned[:, t, :], place(vs_dealt, t), ident[:])
         vs_cols = keep.tile([P, PACK], F32, name="vs_cols")
         nc.scalar.copy(vs_cols[:], vs_turned[:, :, ROW])
 
@@ -147,13 +151,17 @@ def tile_attend_soft_draft_sink_topkq128n512t2048_kernel(
         def pick_values(h, slot, identity_slot):
             picked = keep.tile([P, N], BF16, name="picked%d" % h, tag=slot, align_bytes=64)
             nc.vector.tensor_copy(dealt(picked[:]), value_pools[h][:].indirect(listed))
-            ident_bf = keep.tile([P, P], BF16, name="ident_bf%d" % h, tag=identity_slot, align_bytes=64)
-            nc.scalar.copy(ident_bf[:], ident[:])
-            turned = psum.tile([P, PACK, P], BF16, name="turned%d" % h, tag="bank%d" % (2 - 2 * h))
-            for t in range(PACK):
-                nc.tensor.transpose(turned[:, t, :], picked[:, t * P : (t + 1) * P], ident_bf[:])
+            own_ident = keep.tile([P, P], F32, name="own_ident%d" % h, tag=identity_slot, align_bytes=64)
+            nc.scalar.copy(own_ident[:], ident[:])
+            words = picked[:].bitcast(F32)
+            turned = psum.tile([P, 2, P], F32, name="turned%d" % h, tag="bank%d" % (2 - 2 * h))
+            for u in range(2):
+                nc.tensor.transpose(turned[:, u, :], words[:, u * P : (u + 1) * P], own_ident[:])
             packed = keep.tile([P, P, PACK], BF16, name="packed%d" % h, align_bytes=64)
-            nc.scalar.copy(packed[:], turned[:].rearrange("s t e -> s e t"))
+            nc.scalar.copy(
+                packed[:].rearrange("s e t -> s (e t)").bitcast(F32).rearrange("s (e u) -> s e u", u=2),
+                turned[:].rearrange("s u e -> s e u"),
+            )
             return packed
 
         v_packed = [pick_values(0, "chain_d", "key_codes1")]
@@ -171,13 +179,21 @@ def tile_attend_soft_draft_sink_topkq128n512t2048_kernel(
             accum_out=neg_max[:],
         )
         prob = keep.tile([P, N + 8], F32, name="prob")
-        total = keep.tile([P, 1], F32, name="total")
-        nc.scalar.activation(
-            prob[:, 0 : N + 1], neg_score[:, 0 : N + 1], ACT.Exp, bias=neg_max[:], scale=-1.0, accum_out=total[:]
-        )
         prob_turned = psum.tile([P, PACK, NQ], F32, name="prob_turned", tag="bank1")
-        for t in range(PACK):
-            nc.tensor.transpose(prob_turned[:, t, :], prob[:, t * P : (t + 1) * P], ident[:])
+        sums = []
+        for part, (first, last) in enumerate(((0, N // 2), (N // 2, N + 1))):
+            part_sum = keep.tile([P, 1], F32, name="part_sum%d" % part)
+            nc.scalar.activation(
+                prob[:, first:last],
+                neg_score[:, first:last],
+                ACT.Exp,
+                bias=neg_max[:],
+                scale=-1.0,
+                accum_out=part_sum[:],
+            )
+            sums.append(part_sum)
+            for t in range(2 * part, 2 * part + 2):
+                nc.tensor.transpose(prob_turned[:, t, :], place(prob, t), ident[:])
 
         v_packed.append(pick_values(1, "chain_a", "row2"))
 
@@ -188,6 +204,8 @@ def tile_attend_soft_draft_sink_topkq128n512t2048_kernel(
             vs_cols[:].unsqueeze(1).to_broadcast([P, NQ, PACK]),
             ALU.mult,
         )
+        total = keep.tile([P, 1], F32, name="total")
+        nc.vector.tensor_tensor(total[:], sums[0][:], sums[1][:], ALU.add)
         inverse = keep.tile([P, 1], F32, name="inverse")
         nc.vector.reciprocal(inverse[:], total[:])
 

from contextlib import ExitStack

import concourse.mybir as mybir
from concourse.masks import make_identity

P = 128
N, T, D, DV, NQ = 512, 2048, 1024, 256, 128
PACK = 4
PASSES = D // (P * PACK)
HALVES = DV // P
FLOPS = 2 * NQ * N * (D + DV)
BYTES = P * T * 4 + 32 * T + D * NQ + 32 * NQ + DV * T * 4 + 2 * T * 4 + 2 * NQ * 4 + P * 64 + NQ * DV * 4

F32 = mybir.dt.float32
BF16 = mybir.dt.bfloat16
I32 = mybir.dt.int32
U32 = mybir.dt.uint32
U16 = mybir.dt.uint16
U8 = mybir.dt.uint8
FP8X4 = mybir.dt.float8_e4m3fn_x4
FP4X4 = mybir.dt.float4_e2m1fn_x4
ALU = mybir.AluOpType
ACT = mybir.ActivationFunctionType

MASKED = 30000.0
STEEP = 2.0 ** 60
LOW = 96
ROW = P - 1


def in_order(row):
    return row.rearrange("x (b u k) -> x b u k", u=2, k=16)


def dealt(row):
    return row.rearrange("x (u b k) -> x b u k", u=2, k=16)


def place(row, t):
    return row[:, (t // 2) * (N // 2) + t % 2 : (t // 2 + 1) * (N // 2) : 2]


def tile_attend_soft_draft_sink_topkq128n512t2048_kernel(
    tc, q_words, q_scales, k_words, k_scales, vT, vs, pos, qpos, sink, offs, out
):
    nc = tc.nc
    with ExitStack() as ctx:
        keep = ctx.enter_context(tc.tile_pool(name="keep", bufs=1))
        psum = ctx.enter_context(tc.psum_pool(name="psum", bufs=1))

        offsets = keep.tile([P, N // 16], U16, name="offsets")
        nc.sync.dma_start(offsets[:], offs)
        listed = offsets[:]

        kscale_pool = keep.tile([P, T], U8, name="kscale_pool")
        nc.sync.dma_start(kscale_pool[LOW:P, :].bitcast(I32), k_scales.rearrange("o f t -> f o t").bitcast(I32))
        pos_parts = keep.tile([P, 4, 4], F32, name="pos_parts", tag="chain_e")
        nc.scalar.dma_start(pos_parts[:], pos[0].rearrange("(p b i) -> p b i", b=4, i=4))
        vs_pool = keep.tile([P, T], F32, name="vs_pool", tag="chain_c", align_bytes=64)
        nc.sync.dma_start(vs_pool[ROW:P, :], vs[0:1, :])
        qpos_col = keep.tile([P, 1], F32, name="qpos_col")
        nc.scalar.dma_start(qpos_col[:], qpos[0])
        q_codes = keep.tile([P, PASSES, NQ], I32, name="q_codes", align_bytes=64)
        nc.scalar.dma_start(q_codes[:], q_words[0].rearrange("o g q r -> g o (q r)").bitcast(I32))
        sink_col = keep.tile([P, 1], F32, name="sink_col")
        nc.scalar.dma_start(sink_col[:], sink[0])
        key_pool = keep.tile([P, T], I32, name="key_pool", tag="chain_b", align_bytes=64)
        nc.sync.dma_start(key_pool[:], k_words[0].rearrange("g t b -> g (t b)").bitcast(I32))

        warm = keep.tile([P, 1], F32, name="warm")
        nc.vector.memset(warm[:], 0.0)
        nc.scalar.activation(warm[:], warm[:], ACT.Exp)

        q_plane = keep.tile([P, PASSES * NQ], U8, name="q_plane", align_bytes=64)
        nc.vector.memset(q_plane[:].bitcast(I32), 0)
        qrows = q_scales[0].rearrange("o (c r) q -> r c o q", r=4)
        for r in range(4):
            nc.sync.dma_start(
                q_plane[r::32, :].bitcast(I32).rearrange("c (o q) -> c o q", o=PASSES),
                qrows[r].bitcast(I32),
            )
        first_values = keep.tile([P, T], F32, name="first_values", tag="chain_a", align_bytes=64)
        nc.sync.dma_start(first_values[:], vT[0:P, :])
        nc.vector.memset(kscale_pool[0:LOW, :].bitcast(I32), 0)
        k_plane = keep.tile([P, PASSES * N], U8, name="k_plane", align_bytes=64)
        nc.vector.memset(k_plane[:].bitcast(I32), 0)
        nc.vector.memset(vs_pool[0:ROW, :].bitcast(I32), 0)

        ident = keep.tile([P, P], F32, name="ident")
        make_identity(nc, ident[:])
        neg_qpos = keep.tile([P, 1], F32, name="neg_qpos")
        nc.scalar.activation(neg_qpos[:], qpos_col[:], ACT.Copy, scale=-1.0)

        pos_pool = keep.tile([P, T], F32, name="pos_pool", tag="chain_d", align_bytes=64)
        for b in range(4):
            spread = psum.tile([P, 4, P], F32, name="spread%d" % b, tag="bank%d" % b)
            for i in range(4):
                nc.tensor.transpose(spread[:, i, :], pos_parts[:, b, i : i + 1].to_broadcast([P, P]), ident[:])
            nc.scalar.copy(
                pos_pool[:].rearrange("q (p b i) -> q b p i", b=4, i=4)[:, b],
                spread[:].rearrange("q i p -> q p i"),
            )

        kscale_rows = keep.tile([P, N], U8, name="kscale_rows")
        nc.vector.tensor_copy(kscale_rows[:], kscale_pool[:].indirect(listed))
        for c in range(4):
            nc.sync.dma_start(
                k_plane[32 * c : 32 * c + 4, :].bitcast(I32).rearrange("r (o n) -> r o n", o=PASSES),
                kscale_rows[LOW + 8 * c : LOW + 8 * c + 8, :].bitcast(I32),
            )

        vs_row = keep.tile([P, N], F32, name="vs_row")
        nc.vector.tensor_copy(vs_row[:], vs_pool[:].indirect(listed))
        vs_dealt = keep.tile([P, N], F32, name="vs_dealt", tag="chain_e")
        nc.scalar.copy(dealt(vs_dealt[:]), in_order(vs_row[:]))
        vs_turned = psum.tile([P, PACK, P], F32, name="vs_turned", tag="bank3")
        for t in range(PACK):
            nc.tensor.transpose(vs_turned[:, t, :], place(vs_dealt, t), ident[:])
        vs_cols = keep.tile([P, PACK], F32, name="vs_cols")
        nc.scalar.copy(vs_cols[:], vs_turned[:, :, ROW])

        second_values = keep.tile([P, T], F32, name="second_values", tag="chain_c", align_bytes=64)
        nc.sync.dma_start(second_values[:], vT[P : 2 * P, :])
        value_pools = [first_values, second_values]

        neg_score = keep.tile([P, N + 8], F32, name="neg_score", tag="row2", align_bytes=64)
        nc.scalar.activation(neg_score[:, N : N + 1], sink_col[:], ACT.Copy, scale=-1.0)

        key_pairs = keep.tile([P, N], U32, name="key_pairs")
        nc.vector.tensor_copy(key_pairs[:], key_pool[:].bitcast(U32).indirect(listed))
        score = psum.tile([P, N], F32, name="score")
        for o in range(PASSES):
            key_codes = keep.tile([P, 2 * N], U8, name="key_codes%d" % o, tag="key_codes%d" % o, align_bytes=64)
            nc.vector.tensor_copy(key_codes[:].bitcast(U16), key_pairs[:].bitcast(U16)[:, o::2])
            nc.tensor.matmul_mx(
                score[:],
                lhsT=q_codes[:, o, :].bitcast(FP8X4),
                lhsT_scale=q_plane[:, o * NQ : (o + 1) * NQ],
                rhs=key_codes[:].bitcast(FP4X4),
                rhs_scale=k_plane[:, o * N : (o + 1) * N],
                start=(o == 0),
                stop=(o == PASSES - 1),
            )

        pos_row = keep.tile([P, N], F32, name="pos_row", tag="chain_b", align_bytes=64)
        nc.vector.tensor_copy(pos_row[:], pos_pool[:].indirect(listed))
        ahead = keep.tile([P, N], F32, name="ahead")
        nc.scalar.activation(ahead[:], pos_row[:], ACT.Relu, bias=neg_qpos[:])


        def pick_values(h, slot, identity_slot):
            picked = keep.tile([P, N], BF16, name="picked%d" % h, tag=slot, align_bytes=64)
            nc.vector.tensor_copy(dealt(picked[:]), value_pools[h][:].indirect(listed))
            own_ident = keep.tile([P, P], F32, name="own_ident%d" % h, tag=identity_slot, align_bytes=64)
            nc.scalar.copy(own_ident[:], ident[:])
            words = picked[:].bitcast(F32)
            turned = psum.tile([P, 2, P], F32, name="turned%d" % h, tag="bank%d" % (2 - 2 * h))
            for u in range(2):
                nc.tensor.transpose(turned[:, u, :], words[:, u * P : (u + 1) * P], own_ident[:])
            packed = keep.tile([P, P, PACK], BF16, name="packed%d" % h, align_bytes=64)
            nc.scalar.copy(
                packed[:].rearrange("s e t -> s (e t)").bitcast(F32).rearrange("s (e u) -> s e u", u=2),
                turned[:].rearrange("s u e -> s e u"),
            )
            return packed

        v_packed = [pick_values(0, "chain_d", "key_codes1")]

        neg_raw = keep.tile([P, N], F32, name="neg_raw", tag="chain_a", align_bytes=64)
        nc.vector.scalar_tensor_tensor(neg_raw[:], ahead[:], STEEP, score[:], ALU.mult, ALU.subtract)
        neg_max = keep.tile([P, 1], F32, name="neg_max", tag="v0_plane", align_bytes=64)
        nc.vector.tensor_scalar(
            dealt(neg_score[:, 0:N]),
            in_order(neg_raw[:]),
            MASKED,
            neg_score[:, N : N + 1],
            ALU.min,
            ALU.min,
            accum_out=neg_max[:],
        )
        prob = keep.tile([P, N + 8], F32, name="prob")
        prob_turned = psum.tile([P, PACK, NQ], F32, name="prob_turned", tag="bank1")
        sums = []
        for part, (first, last) in enumerate(((0, N // 2), (N // 2, N + 1))):
            part_sum = keep.tile([P, 1], F32, name="part_sum%d" % part)
            nc.scalar.activation(
                prob[:, first:last],
                neg_score[:, first:last],
                ACT.Exp,
                bias=neg_max[:],
                scale=-1.0,
                accum_out=part_sum[:],
            )
            sums.append(part_sum)
            for t in range(2 * part, 2 * part + 2):
                nc.tensor.transpose(prob_turned[:, t, :], place(prob, t), ident[:])

        v_packed.append(pick_values(1, "chain_a", "row2"))

        weight = keep.tile([P, NQ, PACK], BF16, name="weight", tag="chain_c", align_bytes=64)
        nc.vector.tensor_tensor(
            weight[:],
            prob_turned[:].rearrange("s t q -> s q t"),
            vs_cols[:].unsqueeze(1).to_broadcast([P, NQ, PACK]),
            ALU.mult,
        )
        total = keep.tile([P, 1], F32, name="total")
        nc.vector.tensor_tensor(total[:], sums[0][:], sums[1][:], ALU.add)
        inverse = keep.tile([P, 1], F32, name="inverse")
        nc.vector.reciprocal(inverse[:], total[:])

        def quantise(values, name):
            codes = keep.tile([P, P], U32, name=name + "_codes", align_bytes=64)
            plane = keep.tile([P, P], U8, name=name + "_plane", tag=name + "_plane", align_bytes=64)
            nc.vector.quantize_mx(codes[:].bitcast(FP8X4), plane[:], values[:].rearrange("s c t -> s (c t)"))
            return codes, plane

        quantised = [quantise(v_packed[0], "v0")]
        w_codes, w_plane = quantise(weight, "w")
        quantised.append(quantise(v_packed[1], "v1"))

        for h, tag in enumerate(("bank_a", "bank_b")):
            codes, plane = quantised[h]
            acc = psum.tile([NQ, P], F32, name="acc%d" % h, tag=tag)
            nc.tensor.matmul_mx(
                acc[:],
                lhsT=w_codes[:].bitcast(FP8X4),
                lhsT_scale=w_plane[:],
                rhs=codes[:].bitcast(FP8X4),
                rhs_scale=plane[:],
                start=True,
                stop=True,
            )
            result = keep.tile([NQ, P], F32, name="result%d" % h)
            if h == 0:
                nc.scalar.activation(result[:], acc[:], ACT.Copy, scale=inverse[:])
                nc.scalar.dma_start(out[0][:, h * P : (h + 1) * P], result[:])
            else:
                nc.vector.tensor_scalar(result[:], acc[:], inverse[:], None, ALU.mult)
                nc.sync.dma_start(out[0][:, h * P : (h + 1) * P], result[:])
